import numpy as np
import ml_dtypes


def mxq(x, axis, fmt="e4m3"):
    dtype, down = {"e4m3": (ml_dtypes.float8_e4m3fn, 7), "e5m2": (ml_dtypes.float8_e5m2, 14)}[fmt]
    v = np.moveaxis(np.asarray(x, np.float32).astype(ml_dtypes.bfloat16).astype(np.float64), axis, -1)
    blocks = v.reshape(v.shape[:-1] + (-1, 32))
    amax = np.abs(blocks).max(-1, keepdims=True)
    byte = np.maximum(np.where(amax > 0, np.frexp(amax)[1] - 1 + 127, 0) - down, 1)
    scale = np.exp2(byte - 127.0)
    codes = (blocks / scale).astype(np.float32).astype(dtype).astype(np.float64)
    return np.moveaxis((codes * scale).reshape(v.shape), -1, axis)


WIDE = False


def mx_kscale(k):
    if not WIDE:
        return np.ones(k)
    levels = np.array([10, -10, 5, -5, 0])
    if k % 512:
        return np.exp2(np.random.permutation(np.resize(levels, k // 32))).repeat(32)
    a = np.empty((k // 512, 16))
    for p in range(k // 512):
        a[p, :8] = np.random.permutation(np.resize(levels, 8))
        for g in range(8):
            far = levels[np.abs(levels - a[p, g]) >= 10]
            a[p, g + 8] = far[np.random.randint(len(far))]
    return np.exp2(a.ravel()).repeat(32)


def f64(x):
    return np.asarray(x).astype(np.float64)


def striped8(idx):
    return np.asarray(idx).reshape(8, -1, 16).transpose(0, 2, 1).reshape(128, -1).astype(np.uint16)


def unstriped8(offs):
    return offs.reshape(8, 16, -1).transpose(0, 2, 1).reshape(8, -1).astype(np.int64)


def pick8(x, idx, run):
    r = np.arange(len(x))
    return x[r[:, None], idx[r % (8 * run) // run]]


E2M1 = np.array([0.0, 0.5, 1.0, 1.5, 2.0, 3.0, 4.0, 6.0, -0.0, -0.5, -1.0, -1.5, -2.0, -3.0, -4.0, -6.0])


def pack_weight(w, fmt):
    k, n = w.shape
    w = f64(np.asarray(w, np.float32).astype(ml_dtypes.bfloat16)).reshape(k // 32, 32, n)
    amax = np.abs(w).max(1)
    if fmt == "e4m3":
        byte = np.frexp(amax)[1] - 1 + 127 - 7
    else:
        mant, ex = np.frexp(amax / 6.0)
        byte = np.where(mant > 0.5, ex, ex - 1) + 127
    byte = np.clip(np.where(amax > 0, byte, 1), 1, 254)
    scaled = (w * np.exp2(127.0 - byte)[:, None, :]).reshape(k, n).astype(np.float32)
    by_word = np.ascontiguousarray(scaled.reshape(k // 512, 128, 4, n).transpose(0, 1, 3, 2))
    if fmt == "e4m3":
        words = by_word.astype(ml_dtypes.float8_e4m3fn).view(np.uint8)
    else:
        c = by_word.astype(ml_dtypes.float4_e2m1fn).view(np.uint8) & 0xF
        words = (c[..., 0::2] | (c[..., 1::2] << 4)).reshape(k // 512, 128, 2 * n)
    return np.ascontiguousarray(words), np.ascontiguousarray(byte.astype(np.uint8).reshape(k // 512, 16, n))


def unpack_weight(words, scales, fmt):
    g, _, n = scales.shape
    words = np.ascontiguousarray(words).reshape(g, 128, n, -1)
    if fmt == "e4m3":
        vals = words.view(ml_dtypes.float8_e4m3fn).astype(np.float64)
    else:
        nib = np.empty((g, 128, n, 4), np.uint8)
        nib[..., 0::2] = words & 0xF
        nib[..., 1::2] = words >> 4
        vals = E2M1[nib]
    vals = vals * np.repeat(np.exp2(scales.astype(np.float64) - 127.0), 8, axis=1)[..., None]
    return vals.transpose(0, 1, 3, 2).reshape(g * 512, n)


D, T, I, Q = 512, 1024, 512, 128


def setup_inputs():
    n = np.random.standard_normal
    idx = np.stack([np.random.permutation(T)[:I] for _ in range(8)])
    idx2 = np.stack([np.random.permutation(T)[:I] for _ in range(8)])
    idx3 = np.stack([np.random.permutation(T)[:I] for _ in range(8)])
    idx4 = np.stack([np.random.permutation(T)[:I] for _ in range(8)])
    fd = mx_kscale(D)
    keysp = pack_weight(n((D, T)) / fd[:, None], "e4m3")
    return {
        "query": (n((D, Q)) * 1.1 / np.sqrt(D) * fd[:, None]).astype(np.float32),
        "keys_words": keysp[0],
        "keys_scales": keysp[1],
        "lam": (np.random.uniform(0.8, 1.5, (Q, 1))).astype(np.float32),
        "old": (1.0 * n((Q, T))).astype(np.float32),
        "offs": striped8(idx),
        "offs2": striped8(idx2),
        "offs3": striped8(idx3),
        "offs4": striped8(idx4),
    }


def reference(query, keys_words, keys_scales, lam, old, offs, offs2, offs3, offs4):
    idx = unstriped8(offs)
    idx2 = unstriped8(offs2)
    idx3 = unstriped8(offs3)
    idx4 = unstriped8(offs4)
    keysu = unpack_weight(keys_words, keys_scales, "e4m3")
    queryq = mxq(f64(query), 0, "e4m3")
    a = queryq.T @ keysu
    lo2 = np.minimum(pick8(a, idx2, 16), pick8(a, idx3, 16)) - 0.5
    hi2 = np.maximum(pick8(a, idx2, 16), pick8(a, idx3, 16)) + 0.5
    w = (pick8(a, idx, 16) - np.maximum(lo2, np.minimum(hi2, pick8(a, idx, 16))) * 0.5) * f64(lam)
    f1 = np.zeros((Q, T))
    f1[np.arange(Q)[:, None], idx4[np.arange(Q) % 128 // 16]] = w
    y = f64(old) + f1
    return y

@@ -1,0 +1,124 @@
+from contextlib import ExitStack
+
+import concourse.mybir as mybir
+
+D, T, I, Q = 512, 1024, 512, 128
+FLOPS = 2 * D * T * Q
+
+F32 = mybir.dt.float32
+BF16 = mybir.dt.bfloat16
+I32 = mybir.dt.int32
+U32 = mybir.dt.uint32
+U16 = mybir.dt.uint16
+U8 = mybir.dt.uint8
+FP8X4 = mybir.dt.float8_e4m3fn_x4
+ALU = mybir.AluOpType
+COPY = mybir.ActivationFunctionType.Copy
+
+P = 128
+PACK = 4
+KEY_LOAD = 512
+N_TILE = 256
+HALF = I // 2
+STORE = 256
+
+
+def tile_attend_heldbetween_lean_putold_heads_kernel(
+    tc, query, keys_words, keys_scales, lam, old, offs, offs2, offs3, offs4, out
+):
+    nc = tc.nc
+    with ExitStack() as ctx:
+        keep = ctx.enter_context(tc.tile_pool(name="keep", bufs=1))
+        psum = ctx.enter_context(tc.psum_pool(name="psum", bufs=1))
+
+        lists = {}
+        for name in ("offs", "offs2", "offs3", "offs4"):
+            lists[name] = keep.tile([P, I // 16], U16, name=name)
+
+        key_scales = keep.tile([P, T], U8, align_bytes=64)
+        nc.vector.memset(key_scales[:].bitcast(I32), 0)
+        placed = keep.tile([P, T], F32)
+        nc.vector.memset(placed[:], 0.0)
+
+        q_raw = keep.tile([P, PACK, Q], F32)
+        nc.sync.dma_start(out=q_raw[:], in_=query.rearrange("(p j) w -> p j w", j=PACK))
+        for quad in range(4):
+            nc.scalar.dma_start(
+                out=key_scales[32 * quad : 32 * quad + 4, :].bitcast(I32),
+                in_=keys_scales[0, 4 * quad : 4 * quad + 4, :].bitcast(I32),
+            )
+        words_hbm = keys_words[0].rearrange("p n t -> p (n t)").bitcast(I32)
+        key_words = []
+        for c in range(T // KEY_LOAD):
+            words = keep.tile([P, KEY_LOAD], U32, name="words%d" % c, align_bytes=64)
+            nc.sync.dma_start(out=words[:].bitcast(I32), in_=words_hbm[:, c * KEY_LOAD : (c + 1) * KEY_LOAD])
+            key_words.append(words)
+        nc.sync.dma_start(lists["offs2"][:], offs2)
+        nc.sync.dma_start(lists["offs3"][:], offs3)
+        nc.sync.dma_start(lists["offs"][:], offs)
+        lam_sb = keep.tile([P, 1], F32)
+        nc.sync.dma_start(out=lam_sb[:], in_=lam)
+        nc.sync.dma_start(lists["offs4"][:], offs4)
+        old_sb = keep.tile([P, T], F32)
+        nc.sync.dma_start(out=old_sb[:], in_=old)
+
+        q_bf = keep.tile([P, Q, PACK], BF16, align_bytes=64)
+        nc.vector.tensor_copy(out=q_bf[:], in_=q_raw[:].rearrange("p j w -> p w j"))
+        q_words = keep.tile([P, Q], U32, align_bytes=64)
+        q_scales = keep.tile([P, Q], U8, align_bytes=64)
+        nc.vector.quantize_mx(
+            out=q_words[:].bitcast(FP8X4), scales=q_scales[:], in_=q_bf[:].rearrange("p w j -> p (w j)")
+        )
+
+        a = keep.tile([P, T], F32)
+        for n in range(T // N_TILE):
+            bank = psum.tile([P, N_TILE], F32, name="bank%d" % n)
+            first = n * N_TILE
+            words = key_words[first // KEY_LOAD]
+            nc.tensor.matmul_mx(
+                out=bank[:],
+                lhsT=q_words[:].bitcast(FP8X4),
+                lhsT_scale=q_scales[:],
+                rhs=words[:, first % KEY_LOAD : first % KEY_LOAD + N_TILE].bitcast(FP8X4),
+                rhs_scale=key_scales[:, first : first + N_TILE],
+                start=True,
+                stop=True,
+            )
+            if n % 2 == 0:
+                nc.scalar.activation(out=a[:, first : first + N_TILE], in_=bank[:], func=COPY)
+            else:
+                nc.vector.tensor_copy(out=a[:, first : first + N_TILE], in_=bank[:])
+
+        halves = [slice(h * HALF, (h + 1) * HALF) for h in range(2)]
+        second = keep.tile([P, I], F32)
+        third = keep.tile([P, I], F32)
+        first_tok = keep.tile([P, I], F32)
+        nc.vector.tensor_copy(second[:], a[:].indirect(lists["offs2"][:]))
+        nc.scalar.activation(third[:], a[:].indirect(lists["offs3"][:]), COPY)
+        for h in range(2):
+            cols = lists["offs"][:, h * HALF // 16 : (h + 1) * HALF // 16]
+            nc.scalar.activation(first_tok[:, halves[h]], a[:].indirect(cols), COPY)
+        scaled_first = keep.tile([P, I], F32)
+        nc.scalar.activation(scaled_first[:], first_tok[:], COPY, scale=lam_sb[:, 0:1])
+
+        larger = keep.tile([P, I], F32)
+        smaller = keep.tile([P, I], F32)
+        capped = keep.tile([P, I], F32)
+        held = keep.tile([P, I], F32)
+        scaled_held = keep.tile([P, I], F32)
+        nc.vector.tensor_tensor(larger[:], second[:], third[:], ALU.max)
+        nc.vector.tensor_tensor(smaller[:], second[:], third[:], ALU.min)
+        for s in halves:
+            nc.vector.scalar_tensor_tensor(capped[:, s], larger[:, s], 0.5, first_tok[:, s], ALU.add, ALU.min)
+        for s in halves:
+            nc.vector.scalar_tensor_tensor(held[:, s], smaller[:, s], -0.5, capped[:, s], ALU.add, ALU.max)
+        for s in halves:
+            nc.vector.tensor_scalar(scaled_held[:, s], held[:, s], lam_sb[:, 0:1], -0.5, ALU.mult, ALU.mult)
+        nc.vector.tensor_tensor(placed[:].indirect(lists["offs4"][:]), scaled_first[:], scaled_held[:], ALU.add)
+
+        for c in range(T // STORE):
+            cols = slice(c * STORE, (c + 1) * STORE)
+            total = keep.tile([P, STORE], F32, name="total%d" % c)
+            nc.vector.tensor_tensor(total[:], placed[:, cols], old_sb[:, cols], ALU.add)
+            queue = nc.sync if c % 2 == 0 else nc.scalar
+            queue.dma_start(out=out[:, cols], in_=total[:])

@@ -18,7 +18,7 @@ COPY = mybir.ActivationFunctionType.Copy
 P = 128
 PACK = 4
 KEY_LOAD = 512
-N_TILE = 256
+PIECES = (256, 256, 256, 128, 128)
 HALF = I // 2
 STORE = 256
 
@@ -63,17 +63,22 @@ def tile_attend_heldbetween_lean_putold_heads_kernel(
         nc.sync.dma_start(out=old_sb[:], in_=old)
 
         q_bf = keep.tile([P, Q, PACK], BF16, align_bytes=64)
-        nc.vector.tensor_copy(out=q_bf[:], in_=q_raw[:].rearrange("p j w -> p w j"))
         q_words = keep.tile([P, Q], U32, align_bytes=64)
         q_scales = keep.tile([P, Q], U8, align_bytes=64)
-        nc.vector.quantize_mx(
-            out=q_words[:].bitcast(FP8X4), scales=q_scales[:], in_=q_bf[:].rearrange("p w j -> p (w j)")
-        )
+        q_halves = [slice(h * Q // 2, (h + 1) * Q // 2) for h in range(2)]
+        for rows in q_halves:
+            nc.vector.tensor_copy(out=q_bf[:, rows, :], in_=q_raw[:, :, rows].rearrange("p j w -> p w j"))
+        for rows in q_halves:
+            nc.vector.quantize_mx(
+                out=q_words[:, rows].bitcast(FP8X4),
+                scales=q_scales[:, rows],
+                in_=q_bf[:, rows, :].rearrange("p w j -> p (w j)"),
+            )
 
         a = keep.tile([P, T], F32)
-        for n in range(T // N_TILE):
+        first = 0
+        for n, N_TILE in enumerate(PIECES):
             bank = psum.tile([P, N_TILE], F32, name="bank%d" % n)
-            first = n * N_TILE
             words = key_words[first // KEY_LOAD]
             nc.tensor.matmul_mx(
                 out=bank[:],
@@ -84,37 +89,65 @@ def tile_attend_heldbetween_lean_putold_heads_kernel(
                 start=True,
                 stop=True,
             )
-            if n % 2 == 0:
+            if n % 2 == 1:
                 nc.scalar.activation(out=a[:, first : first + N_TILE], in_=bank[:], func=COPY)
             else:
                 nc.vector.tensor_copy(out=a[:, first : first + N_TILE], in_=bank[:])
+            first = first + N_TILE
 
         halves = [slice(h * HALF, (h + 1) * HALF) for h in range(2)]
         second = keep.tile([P, I], F32)
         third = keep.tile([P, I], F32)
         first_tok = keep.tile([P, I], F32)
-        nc.vector.tensor_copy(second[:], a[:].indirect(lists["offs2"][:]))
-        nc.scalar.activation(third[:], a[:].indirect(lists["offs3"][:]), COPY)
-        for h in range(2):
-            cols = lists["offs"][:, h * HALF // 16 : (h + 1) * HALF // 16]
-            nc.scalar.activation(first_tok[:, halves[h]], a[:].indirect(cols), COPY)
-        scaled_first = keep.tile([P, I], F32)
-        nc.scalar.activation(scaled_first[:], first_tok[:], COPY, scale=lam_sb[:, 0:1])
+        def listed(name, h):
+            return a[:].indirect(lists[name][:, h * HALF // 16 : (h + 1) * HALF // 16])
 
+        for h in range(2):
+            nc.vector.tensor_copy(second[:, halves[h]], listed("offs2", h))
+            nc.scalar.activation(third[:, halves[h]], listed("offs3", h), COPY)
+        for h in range(2):
+            nc.scalar.activation(first_tok[:, halves[h]], listed("offs", h), COPY)
         larger = keep.tile([P, I], F32)
         smaller = keep.tile([P, I], F32)
         capped = keep.tile([P, I], F32)
         held = keep.tile([P, I], F32)
+        scaled_first = keep.tile([P, I], F32)
         scaled_held = keep.tile([P, I], F32)
-        nc.vector.tensor_tensor(larger[:], second[:], third[:], ALU.max)
-        nc.vector.tensor_tensor(smaller[:], second[:], third[:], ALU.min)
-        for s in halves:
+        s0, s1 = halves
+
+        def upper(s):
+            nc.vector.tensor_tensor(larger[:, s], second[:, s], third[:, s], ALU.max)
+
+        def lower(s):
+            nc.vector.tensor_tensor(smaller[:, s], second[:, s], third[:, s], ALU.min)
+
+        def cap(s):
             nc.vector.scalar_tensor_tensor(capped[:, s], larger[:, s], 0.5, first_tok[:, s], ALU.add, ALU.min)
-        for s in halves:
+
+        def floor(s):
             nc.vector.scalar_tensor_tensor(held[:, s], smaller[:, s], -0.5, capped[:, s], ALU.add, ALU.max)
+
+        def place(h):
+            cols = lists["offs4"][:, h * HALF // 16 : (h + 1) * HALF // 16]
+            s = halves[h]
+            nc.vector.tensor_tensor(placed[:].indirect(cols), scaled_first[:, s], scaled_held[:, s], ALU.add)
+
+        minus_half_lam = keep.tile([P, 1], F32)
+        nc.vector.tensor_scalar(minus_half_lam[:], lam_sb[:], -0.5, None, ALU.mult)
         for s in halves:
-            nc.vector.tensor_scalar(scaled_held[:, s], held[:, s], lam_sb[:, 0:1], -0.5, ALU.mult, ALU.mult)
-        nc.vector.tensor_tensor(placed[:].indirect(lists["offs4"][:]), scaled_first[:], scaled_held[:], ALU.add)
+            nc.scalar.activation(scaled_first[:, s], first_tok[:, s], COPY, scale=lam_sb[:, 0:1])
+        upper(s0)
+        lower(s0)
+        upper(s1)
+        cap(s0)
+        lower(s1)
+        floor(s0)
+        cap(s1)
+        nc.vector.tensor_scalar(scaled_held[:, s0], held[:, s0], minus_half_lam[:, 0:1], None, ALU.mult)
+        floor(s1)
+        nc.scalar.activation(scaled_held[:, s1], held[:, s1], COPY, scale=minus_half_lam[:, 0:1])
+        place(0)
+        place(1)
 
         for c in range(T // STORE):
             cols = slice(c * STORE, (c + 1) * STORE)

@@ -17,10 +17,13 @@ COPY = mybir.ActivationFunctionType.Copy
 
 P = 128
 PACK = 4
-KEY_LOAD = 512
-PIECES = (256, 256, 256, 128, 128)
+QUADRANT = 32
+PER_COLUMN = 16
 HALF = I // 2
-STORE = 256
+MARGIN = 0.5
+
+KEY_LOADS = ((256, 128), (256, 128), (128, 128))
+STORES = (128, 256, 256, 256, 128)
 
 
 def tile_attend_heldbetween_lean_putold_heads_kernel(
@@ -33,7 +36,7 @@ def tile_attend_heldbetween_lean_putold_heads_kernel(
 
         lists = {}
         for name in ("offs", "offs2", "offs3", "offs4"):
-            lists[name] = keep.tile([P, I // 16], U16, name=name)
+            lists[name] = keep.tile([P, I // PER_COLUMN], U16, name=name)
 
         key_scales = keep.tile([P, T], U8, align_bytes=64)
         nc.vector.memset(key_scales[:].bitcast(I32), 0)
@@ -42,17 +45,21 @@ def tile_attend_heldbetween_lean_putold_heads_kernel(
 
         q_raw = keep.tile([P, PACK, Q], F32)
         nc.sync.dma_start(out=q_raw[:], in_=query.rearrange("(p j) w -> p j w", j=PACK))
-        for quad in range(4):
-            nc.scalar.dma_start(
-                out=key_scales[32 * quad : 32 * quad + 4, :].bitcast(I32),
-                in_=keys_scales[0, 4 * quad : 4 * quad + 4, :].bitcast(I32),
-            )
         words_hbm = keys_words[0].rearrange("p n t -> p (n t)").bitcast(I32)
-        key_words = []
-        for c in range(T // KEY_LOAD):
-            words = keep.tile([P, KEY_LOAD], U32, name="words%d" % c, align_bytes=64)
-            nc.sync.dma_start(out=words[:].bitcast(I32), in_=words_hbm[:, c * KEY_LOAD : (c + 1) * KEY_LOAD])
-            key_words.append(words)
+        pass_words = []
+        loaded = 0
+        for load, widths in enumerate(KEY_LOADS):
+            words = keep.tile([P, sum(widths)], U32, name="words%d" % load, align_bytes=64)
+            nc.sync.dma_start(out=words[:].bitcast(I32), in_=words_hbm[:, loaded : loaded + sum(widths)])
+            loaded = loaded + sum(widths)
+            for n in range(len(widths)):
+                pass_words.append(words[:, sum(widths[:n]) : sum(widths[: n + 1])])
+            if load == 0:
+                for quad in range(P // QUADRANT):
+                    nc.sync.dma_start(
+                        out=key_scales[QUADRANT * quad : QUADRANT * quad + 4, :].bitcast(I32),
+                        in_=keys_scales[0, 4 * quad : 4 * quad + 4, :].bitcast(I32),
+                    )
         nc.sync.dma_start(lists["offs2"][:], offs2)
         nc.sync.dma_start(lists["offs3"][:], offs3)
         nc.sync.dma_start(lists["offs"][:], offs)
@@ -65,10 +72,10 @@ def tile_attend_heldbetween_lean_putold_heads_kernel(
         q_bf = keep.tile([P, Q, PACK], BF16, align_bytes=64)
         q_words = keep.tile([P, Q], U32, align_bytes=64)
         q_scales = keep.tile([P, Q], U8, align_bytes=64)
-        q_halves = [slice(h * Q // 2, (h + 1) * Q // 2) for h in range(2)]
-        for rows in q_halves:
-            nc.vector.tensor_copy(out=q_bf[:, rows, :], in_=q_raw[:, :, rows].rearrange("p j w -> p w j"))
-        for rows in q_halves:
+        low_rows, high_rows = slice(0, Q // 2), slice(Q // 2, Q)
+        nc.vector.tensor_copy(out=q_bf[:, low_rows, :], in_=q_raw[:, :, low_rows].rearrange("p j w -> p w j"))
+        nc.scalar.copy(out=q_bf[:, high_rows, :], in_=q_raw[:, :, high_rows].rearrange("p j w -> p w j"))
+        for rows in (low_rows, high_rows):
             nc.vector.quantize_mx(
                 out=q_words[:, rows].bitcast(FP8X4),
                 scales=q_scales[:, rows],
@@ -76,82 +83,89 @@ def tile_attend_heldbetween_lean_putold_heads_kernel(
             )
 
         a = keep.tile([P, T], F32)
-        first = 0
-        for n, N_TILE in enumerate(PIECES):
-            bank = psum.tile([P, N_TILE], F32, name="bank%d" % n)
-            words = key_words[first // KEY_LOAD]
+        done = 0
+        for n, words in enumerate(pass_words):
+            width = words.shape[1]
+            tokens = slice(done, done + width)
+            bank = psum.tile([P, width], F32, name="bank%d" % n)
             nc.tensor.matmul_mx(
                 out=bank[:],
                 lhsT=q_words[:].bitcast(FP8X4),
                 lhsT_scale=q_scales[:],
-                rhs=words[:, first % KEY_LOAD : first % KEY_LOAD + N_TILE].bitcast(FP8X4),
-                rhs_scale=key_scales[:, first : first + N_TILE],
+                rhs=words.bitcast(FP8X4),
+                rhs_scale=key_scales[:, tokens],
                 start=True,
                 stop=True,
             )
             if n % 2 == 1:
-                nc.scalar.activation(out=a[:, first : first + N_TILE], in_=bank[:], func=COPY)
+                nc.scalar.activation(out=a[:, tokens], in_=bank[:], func=COPY)
             else:
-                nc.vector.tensor_copy(out=a[:, first : first + N_TILE], in_=bank[:])
-            first = first + N_TILE
+                nc.vector.tensor_copy(out=a[:, tokens], in_=bank[:])
+            done = done + width
 
-        halves = [slice(h * HALF, (h + 1) * HALF) for h in range(2)]
+        slots = [slice(h * HALF, (h + 1) * HALF) for h in range(2)]
+
+        def offsets(name, h):
+            return lists[name][:, h * HALF // PER_COLUMN : (h + 1) * HALF // PER_COLUMN]
+
         second = keep.tile([P, I], F32)
         third = keep.tile([P, I], F32)
-        first_tok = keep.tile([P, I], F32)
-        def listed(name, h):
-            return a[:].indirect(lists[name][:, h * HALF // 16 : (h + 1) * HALF // 16])
+        first = keep.tile([P, I], F32)
+        for h in range(2):
+            nc.vector.tensor_copy(second[:, slots[h]], a[:].indirect(offsets("offs2", h)))
+            nc.scalar.activation(third[:, slots[h]], a[:].indirect(offsets("offs3", h)), COPY)
+        for h in range(2):
+            nc.scalar.activation(first[:, slots[h]], a[:].indirect(offsets("offs", h)), COPY)
 
-        for h in range(2):
-            nc.vector.tensor_copy(second[:, halves[h]], listed("offs2", h))
-            nc.scalar.activation(third[:, halves[h]], listed("offs3", h), COPY)
-        for h in range(2):
-            nc.scalar.activation(first_tok[:, halves[h]], listed("offs", h), COPY)
         larger = keep.tile([P, I], F32)
         smaller = keep.tile([P, I], F32)
         capped = keep.tile([P, I], F32)
         held = keep.tile([P, I], F32)
         scaled_first = keep.tile([P, I], F32)
         scaled_held = keep.tile([P, I], F32)
-        s0, s1 = halves
 
-        def upper(s):
-            nc.vector.tensor_tensor(larger[:, s], second[:, s], third[:, s], ALU.max)
+        def take_larger(h):
+            nc.vector.tensor_tensor(larger[:, slots[h]], second[:, slots[h]], third[:, slots[h]], ALU.max)
 
-        def lower(s):
-            nc.vector.tensor_tensor(smaller[:, s], second[:, s], third[:, s], ALU.min)
+        def take_smaller(h):
+            nc.vector.tensor_tensor(smaller[:, slots[h]], second[:, slots[h]], third[:, slots[h]], ALU.min)
 
-        def cap(s):
-            nc.vector.scalar_tensor_tensor(capped[:, s], larger[:, s], 0.5, first_tok[:, s], ALU.add, ALU.min)
+        def hold_under_upper_bound(h):
+            nc.vector.scalar_tensor_tensor(
+                capped[:, slots[h]], larger[:, slots[h]], MARGIN, first[:, slots[h]], ALU.add, ALU.min
+            )
 
-        def floor(s):
-            nc.vector.scalar_tensor_tensor(held[:, s], smaller[:, s], -0.5, capped[:, s], ALU.add, ALU.max)
+        def hold_over_lower_bound(h):
+            nc.vector.scalar_tensor_tensor(
+                held[:, slots[h]], smaller[:, slots[h]], -MARGIN, capped[:, slots[h]], ALU.add, ALU.max
+            )
 
         def place(h):
-            cols = lists["offs4"][:, h * HALF // 16 : (h + 1) * HALF // 16]
-            s = halves[h]
-            nc.vector.tensor_tensor(placed[:].indirect(cols), scaled_first[:, s], scaled_held[:, s], ALU.add)
+            nc.vector.tensor_tensor(
+                placed[:].indirect(offsets("offs4", h)), scaled_first[:, slots[h]], scaled_held[:, slots[h]], ALU.add
+            )
 
         minus_half_lam = keep.tile([P, 1], F32)
         nc.vector.tensor_scalar(minus_half_lam[:], lam_sb[:], -0.5, None, ALU.mult)
-        for s in halves:
-            nc.scalar.activation(scaled_first[:, s], first_tok[:, s], COPY, scale=lam_sb[:, 0:1])
-        upper(s0)
-        lower(s0)
-        upper(s1)
-        cap(s0)
-        lower(s1)
-        floor(s0)
-        cap(s1)
-        nc.vector.tensor_scalar(scaled_held[:, s0], held[:, s0], minus_half_lam[:, 0:1], None, ALU.mult)
-        floor(s1)
-        nc.scalar.activation(scaled_held[:, s1], held[:, s1], COPY, scale=minus_half_lam[:, 0:1])
+        for h in range(2):
+            nc.scalar.activation(scaled_first[:, slots[h]], first[:, slots[h]], COPY, scale=lam_sb[:, 0:1])
+
+        take_larger(0)
+        take_smaller(0)
+        take_larger(1)
+        hold_under_upper_bound(0)
+        take_smaller(1)
+        hold_over_lower_bound(0)
+        hold_under_upper_bound(1)
+        nc.vector.tensor_scalar(scaled_held[:, slots[0]], held[:, slots[0]], minus_half_lam[:, 0:1], None, ALU.mult)
+        hold_over_lower_bound(1)
+        nc.scalar.activation(scaled_held[:, slots[1]], held[:, slots[1]], COPY, scale=minus_half_lam[:, 0:1])
         place(0)
         place(1)
 
-        for c in range(T // STORE):
-            cols = slice(c * STORE, (c + 1) * STORE)
-            total = keep.tile([P, STORE], F32, name="total%d" % c)
-            nc.vector.tensor_tensor(total[:], placed[:, cols], old_sb[:, cols], ALU.add)
-            queue = nc.sync if c % 2 == 0 else nc.scalar
-            queue.dma_start(out=out[:, cols], in_=total[:])
+        for n, width in enumerate(STORES):
+            tokens = slice(sum(STORES[:n]), sum(STORES[: n + 1]))
+            total = keep.tile([P, width], F32, name="total%d" % n)
+            nc.vector.tensor_tensor(total[:], placed[:, tokens], old_sb[:, tokens], ALU.add)
+            queue = nc.sync if n % 2 == 0 else nc.scalar
+            queue.dma_start(out=out[:, tokens], in_=total[:])

from contextlib import ExitStack

import concourse.mybir as mybir

D, T, I, Q = 512, 1024, 512, 128
FLOPS = 2 * D * T * Q

F32 = mybir.dt.float32
BF16 = mybir.dt.bfloat16
I32 = mybir.dt.int32
U32 = mybir.dt.uint32
U16 = mybir.dt.uint16
U8 = mybir.dt.uint8
FP8X4 = mybir.dt.float8_e4m3fn_x4
ALU = mybir.AluOpType
COPY = mybir.ActivationFunctionType.Copy

P = 128
PACK = 4
QUADRANT = 32
PER_COLUMN = 16
HALF = I // 2
MARGIN = 0.5

KEY_LOADS = ((256, 128), (256, 128), (128, 128))
STORES = (128, 256, 256, 256, 128)


def tile_attend_heldbetween_lean_putold_heads_kernel(
    tc, query, keys_words, keys_scales, lam, old, offs, offs2, offs3, offs4, out
):
    nc = tc.nc
    with ExitStack() as ctx:
        keep = ctx.enter_context(tc.tile_pool(name="keep", bufs=1))
        psum = ctx.enter_context(tc.psum_pool(name="psum", bufs=1))

        lists = {}
        for name in ("offs", "offs2", "offs3", "offs4"):
            lists[name] = keep.tile([P, I // PER_COLUMN], U16, name=name)

        key_scales = keep.tile([P, T], U8, align_bytes=64)
        nc.vector.memset(key_scales[:].bitcast(I32), 0)
        placed = keep.tile([P, T], F32)
        nc.vector.memset(placed[:], 0.0)

        q_raw = keep.tile([P, PACK, Q], F32)
        nc.sync.dma_start(out=q_raw[:], in_=query.rearrange("(p j) w -> p j w", j=PACK))
        words_hbm = keys_words[0].rearrange("p n t -> p (n t)").bitcast(I32)
        pass_words = []
        loaded = 0
        for load, widths in enumerate(KEY_LOADS):
            words = keep.tile([P, sum(widths)], U32, name="words%d" % load, align_bytes=64)
            nc.sync.dma_start(out=words[:].bitcast(I32), in_=words_hbm[:, loaded : loaded + sum(widths)])
            loaded = loaded + sum(widths)
            for n in range(len(widths)):
                pass_words.append(words[:, sum(widths[:n]) : sum(widths[: n + 1])])
            if load == 0:
                for quad in range(P // QUADRANT):
                    nc.sync.dma_start(
                        out=key_scales[QUADRANT * quad : QUADRANT * quad + 4, :].bitcast(I32),
                        in_=keys_scales[0, 4 * quad : 4 * quad + 4, :].bitcast(I32),
                    )
        nc.sync.dma_start(lists["offs2"][:], offs2)
        nc.sync.dma_start(lists["offs3"][:], offs3)
        nc.sync.dma_start(lists["offs"][:], offs)
        lam_sb = keep.tile([P, 1], F32)
        nc.sync.dma_start(out=lam_sb[:], in_=lam)
        nc.sync.dma_start(lists["offs4"][:], offs4)
        old_sb = keep.tile([P, T], F32)
        nc.sync.dma_start(out=old_sb[:], in_=old)

        q_bf = keep.tile([P, Q, PACK], BF16, align_bytes=64)
        q_words = keep.tile([P, Q], U32, align_bytes=64)
        q_scales = keep.tile([P, Q], U8, align_bytes=64)
        low_rows, high_rows = slice(0, Q // 2), slice(Q // 2, Q)
        nc.vector.tensor_copy(out=q_bf[:, low_rows, :], in_=q_raw[:, :, low_rows].rearrange("p j w -> p w j"))
        nc.scalar.copy(out=q_bf[:, high_rows, :], in_=q_raw[:, :, high_rows].rearrange("p j w -> p w j"))
        for rows in (low_rows, high_rows):
            nc.vector.quantize_mx(
                out=q_words[:, rows].bitcast(FP8X4),
                scales=q_scales[:, rows],
                in_=q_bf[:, rows, :].rearrange("p w j -> p (w j)"),
            )

        a = keep.tile([P, T], F32)
        done = 0
        for n, words in enumerate(pass_words):
            width = words.shape[1]
            tokens = slice(done, done + width)
            bank = psum.tile([P, width], F32, name="bank%d" % n)
            nc.tensor.matmul_mx(
                out=bank[:],
                lhsT=q_words[:].bitcast(FP8X4),
                lhsT_scale=q_scales[:],
                rhs=words.bitcast(FP8X4),
                rhs_scale=key_scales[:, tokens],
                start=True,
                stop=True,
            )
            if n % 2 == 1:
                nc.scalar.activation(out=a[:, tokens], in_=bank[:], func=COPY)
            else:
                nc.vector.tensor_copy(out=a[:, tokens], in_=bank[:])
            done = done + width

        slots = [slice(h * HALF, (h + 1) * HALF) for h in range(2)]

        def offsets(name, h):
            return lists[name][:, h * HALF // PER_COLUMN : (h + 1) * HALF // PER_COLUMN]

        second = keep.tile([P, I], F32)
        third = keep.tile([P, I], F32)
        first = keep.tile([P, I], F32)
        for h in range(2):
            nc.vector.tensor_copy(second[:, slots[h]], a[:].indirect(offsets("offs2", h)))
            nc.scalar.activation(third[:, slots[h]], a[:].indirect(offsets("offs3", h)), COPY)
        for h in range(2):
            nc.scalar.activation(first[:, slots[h]], a[:].indirect(offsets("offs", h)), COPY)

        larger = keep.tile([P, I], F32)
        smaller = keep.tile([P, I], F32)
        capped = keep.tile([P, I], F32)
        held = keep.tile([P, I], F32)
        scaled_first = keep.tile([P, I], F32)
        scaled_held = keep.tile([P, I], F32)

        def take_larger(h):
            nc.vector.tensor_tensor(larger[:, slots[h]], second[:, slots[h]], third[:, slots[h]], ALU.max)

        def take_smaller(h):
            nc.vector.tensor_tensor(smaller[:, slots[h]], second[:, slots[h]], third[:, slots[h]], ALU.min)

        def hold_under_upper_bound(h):
            nc.vector.scalar_tensor_tensor(
                capped[:, slots[h]], larger[:, slots[h]], MARGIN, first[:, slots[h]], ALU.add, ALU.min
            )

        def hold_over_lower_bound(h):
            nc.vector.scalar_tensor_tensor(
                held[:, slots[h]], smaller[:, slots[h]], -MARGIN, capped[:, slots[h]], ALU.add, ALU.max
            )

        def place(h):
            nc.vector.tensor_tensor(
                placed[:].indirect(offsets("offs4", h)), scaled_first[:, slots[h]], scaled_held[:, slots[h]], ALU.add
            )

        minus_half_lam = keep.tile([P, 1], F32)
        nc.vector.tensor_scalar(minus_half_lam[:], lam_sb[:], -0.5, None, ALU.mult)
        for h in range(2):
            nc.scalar.activation(scaled_first[:, slots[h]], first[:, slots[h]], COPY, scale=lam_sb[:, 0:1])

        take_larger(0)
        take_smaller(0)
        take_larger(1)
        hold_under_upper_bound(0)
        take_smaller(1)
        hold_over_lower_bound(0)
        hold_under_upper_bound(1)
        nc.vector.tensor_scalar(scaled_held[:, slots[0]], held[:, slots[0]], minus_half_lam[:, 0:1], None, ALU.mult)
        hold_over_lower_bound(1)
        nc.scalar.activation(scaled_held[:, slots[1]], held[:, slots[1]], COPY, scale=minus_half_lam[:, 0:1])
        place(0)
        place(1)

        for n, width in enumerate(STORES):
            tokens = slice(sum(STORES[:n]), sum(STORES[: n + 1]))
            total = keep.tile([P, width], F32, name="total%d" % n)
            nc.vector.tensor_tensor(total[:], placed[:, tokens], old_sb[:, tokens], ALU.add)
            queue = nc.sync if n % 2 == 0 else nc.scalar
            queue.dma_start(out=out[:, tokens], in_=total[:])
